import numpy as np
import ml_dtypes


def mxq(x, axis, fmt="e4m3"):
    dtype, down = {"e4m3": (ml_dtypes.float8_e4m3fn, 7), "e5m2": (ml_dtypes.float8_e5m2, 14)}[fmt]
    v = np.moveaxis(np.asarray(x, np.float32).astype(ml_dtypes.bfloat16).astype(np.float64), axis, -1)
    blocks = v.reshape(v.shape[:-1] + (-1, 32))
    amax = np.abs(blocks).max(-1, keepdims=True)
    byte = np.maximum(np.where(amax > 0, np.frexp(amax)[1] - 1 + 127, 0) - down, 1)
    scale = np.exp2(byte - 127.0)
    codes = (blocks / scale).astype(np.float32).astype(dtype).astype(np.float64)
    return np.moveaxis((codes * scale).reshape(v.shape), -1, axis)


WIDE = False


def mx_kscale(k):
    if not WIDE:
        return np.ones(k)
    levels = np.array([10, -10, 5, -5, 0])
    if k % 512:
        return np.exp2(np.random.permutation(np.resize(levels, k // 32))).repeat(32)
    a = np.empty((k // 512, 16))
    for p in range(k // 512):
        a[p, :8] = np.random.permutation(np.resize(levels, 8))
        for g in range(8):
            far = levels[np.abs(levels - a[p, g]) >= 10]
            a[p, g + 8] = far[np.random.randint(len(far))]
    return np.exp2(a.ravel()).repeat(32)


def f64(x):
    return np.asarray(x).astype(np.float64)


def striped(idx):
    return np.tile(np.asarray(idx).reshape(-1, 16).T, (8, 1)).astype(np.uint16)


def unstriped(offs):
    return offs[:16].T.reshape(-1).astype(np.int64)


E2M1 = np.array([0.0, 0.5, 1.0, 1.5, 2.0, 3.0, 4.0, 6.0, -0.0, -0.5, -1.0, -1.5, -2.0, -3.0, -4.0, -6.0])


def pack_weight(w, fmt):
    k, n = w.shape
    w = f64(np.asarray(w, np.float32).astype(ml_dtypes.bfloat16)).reshape(k // 32, 32, n)
    amax = np.abs(w).max(1)
    if fmt == "e4m3":
        byte = np.frexp(amax)[1] - 1 + 127 - 7
    else:
        mant, ex = np.frexp(amax / 6.0)
        byte = np.where(mant > 0.5, ex, ex - 1) + 127
    byte = np.clip(np.where(amax > 0, byte, 1), 1, 254)
    scaled = (w * np.exp2(127.0 - byte)[:, None, :]).reshape(k, n).astype(np.float32)
    by_word = np.ascontiguousarray(scaled.reshape(k // 512, 128, 4, n).transpose(0, 1, 3, 2))
    if fmt == "e4m3":
        words = by_word.astype(ml_dtypes.float8_e4m3fn).view(np.uint8)
    else:
        c = by_word.astype(ml_dtypes.float4_e2m1fn).view(np.uint8) & 0xF
        words = (c[..., 0::2] | (c[..., 1::2] << 4)).reshape(k // 512, 128, 2 * n)
    return np.ascontiguousarray(words), np.ascontiguousarray(byte.astype(np.uint8).reshape(k // 512, 16, n))


def unpack_weight(words, scales, fmt):
    g, _, n = scales.shape
    words = np.ascontiguousarray(words).reshape(g, 128, n, -1)
    if fmt == "e4m3":
        vals = words.view(ml_dtypes.float8_e4m3fn).astype(np.float64)
    else:
        nib = np.empty((g, 128, n, 4), np.uint8)
        nib[..., 0::2] = words & 0xF
        nib[..., 1::2] = words >> 4
        vals = E2M1[nib]
    vals = vals * np.repeat(np.exp2(scales.astype(np.float64) - 127.0), 8, axis=1)[..., None]
    return vals.transpose(0, 1, 3, 2).reshape(g * 512, n)


B, N, T, D, NQ = 1, 512, 2048, 512, 256


def setup_inputs():
    n = np.random.standard_normal
    idx = np.random.permutation(T)[:B * N]
    s = mx_kscale(D)[:, None]
    kp = pack_weight(n((D, T)) / s, "e4m3")
    return {
        "qT": (n((B, D, NQ)) * s * (0.50 / np.sqrt(D))).astype(np.float32),
        "k_words": kp[0],
        "k_scales": kp[1],
        "kb": np.tile(n(2048), (128, 1)).astype(np.float32),
        "ex": (np.random.uniform(0.5, 2.0, (B, NQ, 1))).astype(np.float32),
        "offs": striped(idx),
    }


def reference(qT, k_words, k_scales, kb, ex, offs):
    idx = unstriped(offs)
    pick = lambda x, which: x[:, which].reshape(x.shape[0], B, -1).transpose(1, 0, 2)
    k = unpack_weight(k_words, k_scales, "e4m3")
    kg = pick(k, idx)
    qq = mxq(f64(qT), 1, "e4m3")
    a = qq.transpose(0, 2, 1) @ kg
    y = np.exp(a + pick(f64(kb), idx)[:, :1, :]) * f64(ex)
    return y

@@ -1,0 +1,127 @@
+from contextlib import ExitStack
+
+import concourse.mybir as mybir
+from concourse.masks import make_identity
+
+D, NQ, T, N = 512, 256, 2048, 512
+FLOPS = 2 * D * NQ * N
+BYTES = 4 * D * NQ + D * T + (D // 32) * T + 4 * T + 4 * NQ + 2 * 128 * (N // 16) + 4 * NQ * N
+
+F32 = mybir.dt.float32
+BF16 = mybir.dt.bfloat16
+I32 = mybir.dt.int32
+U32 = mybir.dt.uint32
+U16 = mybir.dt.uint16
+U8 = mybir.dt.uint8
+FP8X4 = mybir.dt.float8_e4m3fn_x4
+EXP = mybir.ActivationFunctionType.Exp
+ADD = mybir.AluOpType.add
+MULT = mybir.AluOpType.mult
+
+P = 128
+PACK = 4
+HALF = N // 2
+LIST_COLS = N // 16
+
+
+def tile_attend_rate_topk_kernel(tc, qT, k_words, k_scales, kb, ex, offs, out):
+    nc = tc.nc
+    with ExitStack() as ctx:
+        sb = ctx.enter_context(tc.tile_pool(name="sb", bufs=1))
+        ps = ctx.enter_context(tc.psum_pool(name="ps", bufs=1))
+
+        offsets = sb.tile([P, LIST_COLS], U16, name="offsets")
+        nc.sync.dma_start(offsets[:], offs)
+
+        scales = sb.tile([P, T], U8, name="scales", align_bytes=64)
+        nc.sync.dma_start(out=scales[48:64, :].bitcast(I32), in_=k_scales[0].bitcast(I32))
+        bias_row = sb.tile([P, T], F32, name="bias_row", align_bytes=64)
+        nc.sync.dma_start(out=bias_row[P - 1 : P, :], in_=kb[0:1, :])
+        q_raw = sb.tile([P, PACK, NQ], F32, name="q_raw")
+        nc.sync.dma_start(out=q_raw[:], in_=qT[0].rearrange("(p j) q -> p j q", j=PACK))
+        words = sb.tile([P, T], I32, name="words", align_bytes=64)
+        nc.sync.dma_start(out=words[:], in_=k_words[0].rearrange("p t r -> p (t r)").bitcast(I32))
+        expo = sb.tile([P, 2], F32, name="expo")
+        with nc.allow_non_contiguous_dma(reason="one exposure a partition"):
+            nc.sync.dma_start(out=expo[:], in_=ex[0].rearrange("(t p) o -> p (t o)", p=P))
+
+        nc.vector.memset(scales[0:48, :].bitcast(I32), 0)
+        nc.vector.memset(scales[64:P, :].bitcast(I32), 0)
+        nc.vector.memset(bias_row[0 : P - 1, :].bitcast(I32), 0)
+        k_sc = sb.tile([P, N], U8, name="k_sc", align_bytes=64)
+        nc.gpsimd.memset(k_sc[:].bitcast(I32), 0)
+
+        listed_sc = sb.tile([P, N], U8, name="listed_sc", align_bytes=64)
+        nc.vector.tensor_copy(listed_sc[:], scales[:].indirect(offsets[:]))
+        for quad in range(4):
+            nc.sync.dma_start(
+                out=k_sc[32 * quad : 32 * quad + 4, :].bitcast(I32),
+                in_=listed_sc[48 + 4 * quad : 52 + 4 * quad, :].bitcast(I32),
+            )
+
+        ident = sb.tile([P, P], F32, name="ident")
+        make_identity(nc, ident[:])
+        warm = sb.tile([P, 1], F32, name="warm")
+        nc.scalar.activation(warm[:], ident[:, 0:1], EXP)
+
+        def half_list(h):
+            return offsets[:, h * (LIST_COLS // 2) : (h + 1) * (LIST_COLS // 2)]
+
+        q_bf = sb.tile([P, NQ, PACK], BF16, name="q_bf", align_bytes=64)
+        nc.scalar.copy(q_bf[:], q_raw[:].rearrange("p j q -> p q j"))
+
+        bias_all = []
+        for h in range(2):
+            bias_listed = sb.tile([P, HALF], F32, name=f"bias_listed{h}")
+            nc.vector.tensor_copy(bias_listed[:], bias_row[:].indirect(half_list(h)))
+            turned = ps.tile([P, 2, P], F32, name="turned")
+            for s in range(2):
+                nc.tensor.transpose(turned[:, s, :], bias_listed[:, s * P : (s + 1) * P], ident[:])
+            bias_col = sb.tile([P, 2], F32, name=f"bias_col{h}")
+            nc.scalar.copy(bias_col[:], turned[:, :, P - 1])
+            spread = ps.tile([P, 2, P], F32, name=f"spread{h}")
+            for s in range(2):
+                nc.tensor.transpose(spread[:, s, :], bias_col[:, s : s + 1].to_broadcast([P, P]), ident[:])
+            bias_h = sb.tile([P, HALF], F32, name=f"bias_all{h}")
+            nc.scalar.copy(bias_h[:], spread[:].rearrange("p s c -> p (s c)"))
+            bias_all.append(bias_h)
+
+        q_codes = sb.tile([P, NQ], U32, name="q_codes", align_bytes=64)
+        q_sc = sb.tile([P, NQ], U8, name="q_sc", align_bytes=64)
+        nc.vector.quantize_mx(
+            out=q_codes[:].bitcast(FP8X4), scales=q_sc[:], in_=q_bf[:].rearrange("p q j -> p (q j)")
+        )
+
+        pieces = []
+        for h in range(2):
+            k_codes = sb.tile([P, HALF], U32, name=f"k_codes{h}", align_bytes=64)
+            nc.vector.tensor_copy(k_codes[:], words[:].bitcast(U32).indirect(half_list(h)))
+            for t in range(2):
+                rows = slice(t * P, (t + 1) * P)
+                width = P if (h, t) == (1, 1) else HALF
+                for c0 in range(0, HALF, width):
+                    score = ps.tile([P, width], F32, name=f"score{h}{t}{c0}")
+                    nc.tensor.matmul_mx(
+                        out=score[:],
+                        lhsT=q_codes[:, rows].bitcast(FP8X4),
+                        lhsT_scale=q_sc[:, rows],
+                        rhs=k_codes[:, c0 : c0 + width].bitcast(FP8X4),
+                        rhs_scale=k_sc[:, h * HALF + c0 : h * HALF + c0 + width],
+                        start=True,
+                        stop=True,
+                    )
+                    pieces.append((h, t, c0, width, score))
+
+        rates = []
+        for h, t, c0, width, score in pieces:
+            logit = sb.tile([P, width], F32, name=f"logit{h}{t}{c0}")
+            nc.vector.tensor_tensor(logit[:], score[:], bias_all[h][:, c0 : c0 + width], ADD)
+            rate = sb.tile([P, width], F32, name=f"rate{h}{t}{c0}")
+            nc.scalar.activation(rate[:], logit[:], EXP)
+            rates.append((h, t, c0, width, rate))
+        for h, t, c0, width, rate in rates:
+            res = sb.tile([P, width], F32, name=f"res{h}{t}{c0}")
+            nc.vector.tensor_scalar(res[:], rate[:], expo[:, t : t + 1], None, MULT)
+            nc.sync.dma_start(
+                out=out[0, t * P : (t + 1) * P, h * HALF + c0 : h * HALF + c0 + width], in_=res[:]
+            )

@@ -35,7 +35,7 @@ def tile_attend_rate_topk_kernel(tc, qT, k_words, k_scales, kb, ex, offs, out):
 
         scales = sb.tile([P, T], U8, name="scales", align_bytes=64)
         nc.sync.dma_start(out=scales[48:64, :].bitcast(I32), in_=k_scales[0].bitcast(I32))
-        bias_row = sb.tile([P, T], F32, name="bias_row", align_bytes=64)
+        bias_row = sb.tile([P, T], F32, name="bias_row", tag="bias_slot", align_bytes=64)
         nc.sync.dma_start(out=bias_row[P - 1 : P, :], in_=kb[0:1, :])
         q_raw = sb.tile([P, PACK, NQ], F32, name="q_raw")
         nc.sync.dma_start(out=q_raw[:], in_=qT[0].rearrange("(p j) q -> p j q", j=PACK))
@@ -45,11 +45,18 @@ def tile_attend_rate_topk_kernel(tc, qT, k_words, k_scales, kb, ex, offs, out):
         with nc.allow_non_contiguous_dma(reason="one exposure a partition"):
             nc.sync.dma_start(out=expo[:], in_=ex[0].rearrange("(t p) o -> p (t o)", p=P))
 
+        seed = sb.tile([P, 1], F32, name="seed")
+        nc.vector.memset(seed[:], 0.0)
         nc.vector.memset(scales[0:48, :].bitcast(I32), 0)
         nc.vector.memset(scales[64:P, :].bitcast(I32), 0)
-        nc.vector.memset(bias_row[0 : P - 1, :].bitcast(I32), 0)
+        ident = sb.tile([P, P], F32, name="ident")
+        make_identity(nc, ident[:])
         k_sc = sb.tile([P, N], U8, name="k_sc", align_bytes=64)
-        nc.gpsimd.memset(k_sc[:].bitcast(I32), 0)
+        nc.vector.memset(bias_row[0 : P - 1, :], 0.0)
+        nc.vector.memset(k_sc[:].bitcast(I32), 0)
+
+        warm = sb.tile([P, 1], F32, name="warm")
+        nc.scalar.activation(warm[:], seed[:], EXP)
 
         listed_sc = sb.tile([P, N], U8, name="listed_sc", align_bytes=64)
         nc.vector.tensor_copy(listed_sc[:], scales[:].indirect(offsets[:]))
@@ -59,53 +66,48 @@ def tile_attend_rate_topk_kernel(tc, qT, k_words, k_scales, kb, ex, offs, out):
                 in_=listed_sc[48 + 4 * quad : 52 + 4 * quad, :].bitcast(I32),
             )
 
-        ident = sb.tile([P, P], F32, name="ident")
-        make_identity(nc, ident[:])
-        warm = sb.tile([P, 1], F32, name="warm")
-        nc.scalar.activation(warm[:], ident[:, 0:1], EXP)
-
         def half_list(h):
             return offsets[:, h * (LIST_COLS // 2) : (h + 1) * (LIST_COLS // 2)]
 
-        q_bf = sb.tile([P, NQ, PACK], BF16, name="q_bf", align_bytes=64)
+        q_bf = sb.tile([P, NQ, PACK], BF16, name="q_bf", tag="operand_slot", align_bytes=64)
         nc.scalar.copy(q_bf[:], q_raw[:].rearrange("p j q -> p q j"))
 
         bias_all = []
         for h in range(2):
             bias_listed = sb.tile([P, HALF], F32, name=f"bias_listed{h}")
             nc.vector.tensor_copy(bias_listed[:], bias_row[:].indirect(half_list(h)))
-            turned = ps.tile([P, 2, P], F32, name="turned")
+            turned = ps.tile([P, 2, P], F32, name="turned", tag=f"bias_bank{h}")
             for s in range(2):
                 nc.tensor.transpose(turned[:, s, :], bias_listed[:, s * P : (s + 1) * P], ident[:])
             bias_col = sb.tile([P, 2], F32, name=f"bias_col{h}")
             nc.scalar.copy(bias_col[:], turned[:, :, P - 1])
-            spread = ps.tile([P, 2, P], F32, name=f"spread{h}")
+            spread = ps.tile([P, 2, P], F32, name="spread", tag=f"bias_bank{h}")
             for s in range(2):
                 nc.tensor.transpose(spread[:, s, :], bias_col[:, s : s + 1].to_broadcast([P, P]), ident[:])
             bias_h = sb.tile([P, HALF], F32, name=f"bias_all{h}")
             nc.scalar.copy(bias_h[:], spread[:].rearrange("p s c -> p (s c)"))
             bias_all.append(bias_h)
 
-        q_codes = sb.tile([P, NQ], U32, name="q_codes", align_bytes=64)
+        q_codes = sb.tile([P, NQ], U32, name="q_codes", tag="bias_slot", align_bytes=64)
         q_sc = sb.tile([P, NQ], U8, name="q_sc", align_bytes=64)
         nc.vector.quantize_mx(
             out=q_codes[:].bitcast(FP8X4), scales=q_sc[:], in_=q_bf[:].rearrange("p q j -> p (q j)")
         )
 
         pieces = []
+        k_codes = sb.tile([P, N], U32, name="k_codes", tag="operand_slot", align_bytes=64)
         for h in range(2):
-            k_codes = sb.tile([P, HALF], U32, name=f"k_codes{h}", align_bytes=64)
-            nc.vector.tensor_copy(k_codes[:], words[:].bitcast(U32).indirect(half_list(h)))
+            nc.vector.tensor_copy(k_codes[:, h * HALF : (h + 1) * HALF], words[:].bitcast(U32).indirect(half_list(h)))
             for t in range(2):
                 rows = slice(t * P, (t + 1) * P)
-                width = P if (h, t) == (1, 1) else HALF
+                width = P if h == t else HALF
                 for c0 in range(0, HALF, width):
                     score = ps.tile([P, width], F32, name=f"score{h}{t}{c0}")
                     nc.tensor.matmul_mx(
                         out=score[:],
                         lhsT=q_codes[:, rows].bitcast(FP8X4),
                         lhsT_scale=q_sc[:, rows],
-                        rhs=k_codes[:, c0 : c0 + width].bitcast(FP8X4),
+                        rhs=k_codes[:, h * HALF + c0 : h * HALF + c0 + width].bitcast(FP8X4),
                         rhs_scale=k_sc[:, h * HALF + c0 : h * HALF + c0 + width],
                         start=True,
                         stop=True,

@@ -45,8 +45,6 @@ def tile_attend_rate_topk_kernel(tc, qT, k_words, k_scales, kb, ex, offs, out):
         with nc.allow_non_contiguous_dma(reason="one exposure a partition"):
             nc.sync.dma_start(out=expo[:], in_=ex[0].rearrange("(t p) o -> p (t o)", p=P))
 
-        seed = sb.tile([P, 1], F32, name="seed")
-        nc.vector.memset(seed[:], 0.0)
         nc.vector.memset(scales[0:48, :].bitcast(I32), 0)
         nc.vector.memset(scales[64:P, :].bitcast(I32), 0)
         ident = sb.tile([P, P], F32, name="ident")
@@ -54,9 +52,6 @@ def tile_attend_rate_topk_kernel(tc, qT, k_words, k_scales, kb, ex, offs, out):
         k_sc = sb.tile([P, N], U8, name="k_sc", align_bytes=64)
         nc.vector.memset(bias_row[0 : P - 1, :], 0.0)
         nc.vector.memset(k_sc[:].bitcast(I32), 0)
-
-        warm = sb.tile([P, 1], F32, name="warm")
-        nc.scalar.activation(warm[:], seed[:], EXP)
 
         listed_sc = sb.tile([P, N], U8, name="listed_sc", align_bytes=64)
         nc.vector.tensor_copy(listed_sc[:], scales[:].indirect(offsets[:]))

@@ -30,13 +30,13 @@ def tile_attend_rate_topk_kernel(tc, qT, k_words, k_scales, kb, ex, offs, out):
         sb = ctx.enter_context(tc.tile_pool(name="sb", bufs=1))
         ps = ctx.enter_context(tc.psum_pool(name="ps", bufs=1))
 
+        bias_row = sb.tile([P, T], F32, name="bias_row", tag="bias_slot", align_bytes=64)
+        nc.sync.dma_start(out=bias_row[P - 1 : P, :], in_=kb[0:1, :])
         offsets = sb.tile([P, LIST_COLS], U16, name="offsets")
         nc.sync.dma_start(offsets[:], offs)
 
         scales = sb.tile([P, T], U8, name="scales", align_bytes=64)
-        nc.sync.dma_start(out=scales[48:64, :].bitcast(I32), in_=k_scales[0].bitcast(I32))
-        bias_row = sb.tile([P, T], F32, name="bias_row", tag="bias_slot", align_bytes=64)
-        nc.sync.dma_start(out=bias_row[P - 1 : P, :], in_=kb[0:1, :])
+        nc.scalar.dma_start(out=scales[48:64, :].bitcast(I32), in_=k_scales[0].bitcast(I32))
         q_raw = sb.tile([P, PACK, NQ], F32, name="q_raw")
         nc.sync.dma_start(out=q_raw[:], in_=qT[0].rearrange("(p j) q -> p j q", j=PACK))
         words = sb.tile([P, T], I32, name="words", align_bytes=64)
@@ -51,7 +51,6 @@ def tile_attend_rate_topk_kernel(tc, qT, k_words, k_scales, kb, ex, offs, out):
         make_identity(nc, ident[:])
         k_sc = sb.tile([P, N], U8, name="k_sc", align_bytes=64)
         nc.vector.memset(bias_row[0 : P - 1, :], 0.0)
-        nc.vector.memset(k_sc[:].bitcast(I32), 0)
 
         listed_sc = sb.tile([P, N], U8, name="listed_sc", align_bytes=64)
         nc.vector.tensor_copy(listed_sc[:], scales[:].indirect(offsets[:]))

@@ -31,12 +31,12 @@ def tile_attend_rate_topk_kernel(tc, qT, k_words, k_scales, kb, ex, offs, out):
         ps = ctx.enter_context(tc.psum_pool(name="ps", bufs=1))
 
         bias_row = sb.tile([P, T], F32, name="bias_row", tag="bias_slot", align_bytes=64)
-        nc.sync.dma_start(out=bias_row[P - 1 : P, :], in_=kb[0:1, :])
+        nc.scalar.dma_start(out=bias_row[P - 1 : P, :], in_=kb[0:1, :])
+        scales = sb.tile([P, T], U8, name="scales", align_bytes=64)
+        nc.sync.dma_start(out=scales[48:64, :].bitcast(I32), in_=k_scales[0].bitcast(I32))
         offsets = sb.tile([P, LIST_COLS], U16, name="offsets")
         nc.sync.dma_start(offsets[:], offs)
 
-        scales = sb.tile([P, T], U8, name="scales", align_bytes=64)
-        nc.scalar.dma_start(out=scales[48:64, :].bitcast(I32), in_=k_scales[0].bitcast(I32))
         q_raw = sb.tile([P, PACK, NQ], F32, name="q_raw")
         nc.sync.dma_start(out=q_raw[:], in_=qT[0].rearrange("(p j) q -> p j q", j=PACK))
         words = sb.tile([P, T], I32, name="words", align_bytes=64)

@@ -88,36 +88,60 @@ def tile_attend_rate_topk_kernel(tc, qT, k_words, k_scales, kb, ex, offs, out):
             out=q_codes[:].bitcast(FP8X4), scales=q_sc[:], in_=q_bf[:].rearrange("p q j -> p (q j)")
         )
 
-        pieces = []
         k_codes = sb.tile([P, N], U32, name="k_codes", tag="operand_slot", align_bytes=64)
+        passes = [(0, 0, 128), (0, 128, 128), (1, 0, 128), (1, 128, 128), (0, 256, 128), (0, 384, 128), (1, 256, 128), (1, 384, 128)]
+        steps = [(0, 0, 128), (0, 128, 128), (1, 0, 128), (1, 128, 128), (0, 256, 128), (0, 384, 128), (1, 256, 128), (1, 384, 128)]
+        stores = [(0, 0, 256), (1, 0, 256), (0, 256, 256), (1, 256, 128), (1, 384, 128)]
+        scores = {}
         for h in range(2):
             nc.vector.tensor_copy(k_codes[:, h * HALF : (h + 1) * HALF], words[:].bitcast(U32).indirect(half_list(h)))
-            for t in range(2):
+            for i, (t, c0, width) in enumerate(passes):
+                if c0 // HALF != h:
+                    continue
                 rows = slice(t * P, (t + 1) * P)
-                width = P if h == t else HALF
-                for c0 in range(0, HALF, width):
-                    score = ps.tile([P, width], F32, name=f"score{h}{t}{c0}")
-                    nc.tensor.matmul_mx(
-                        out=score[:],
-                        lhsT=q_codes[:, rows].bitcast(FP8X4),
-                        lhsT_scale=q_sc[:, rows],
-                        rhs=k_codes[:, h * HALF + c0 : h * HALF + c0 + width].bitcast(FP8X4),
-                        rhs_scale=k_sc[:, h * HALF + c0 : h * HALF + c0 + width],
-                        start=True,
-                        stop=True,
-                    )
-                    pieces.append((h, t, c0, width, score))
+                cols = slice(c0, c0 + width)
+                bank = f"bias_bank{i - 6}" if i >= 6 else f"score{i}"
+                score = ps.tile([P, width], F32, name=f"score{i}", tag=bank)
+                nc.tensor.matmul_mx(
+                    out=score[:],
+                    lhsT=q_codes[:, rows].bitcast(FP8X4),
+                    lhsT_scale=q_sc[:, rows],
+                    rhs=k_codes[:, cols].bitcast(FP8X4),
+                    rhs_scale=k_sc[:, cols],
+                    start=True,
+                    stop=True,
+                )
+                for c in range(0, width, 64):
+                    scores[t, c0 + c] = (score, c)
 
-        rates = []
-        for h, t, c0, width, score in pieces:
-            logit = sb.tile([P, width], F32, name=f"logit{h}{t}{c0}")
-            nc.vector.tensor_tensor(logit[:], score[:], bias_all[h][:, c0 : c0 + width], ADD)
-            rate = sb.tile([P, width], F32, name=f"rate{h}{t}{c0}")
-            nc.scalar.activation(rate[:], logit[:], EXP)
-            rates.append((h, t, c0, width, rate))
-        for h, t, c0, width, rate in rates:
-            res = sb.tile([P, width], F32, name=f"res{h}{t}{c0}")
-            nc.vector.tensor_scalar(res[:], rate[:], expo[:, t : t + 1], None, MULT)
-            nc.sync.dma_start(
-                out=out[0, t * P : (t + 1) * P, h * HALF + c0 : h * HALF + c0 + width], in_=res[:]
-            )
+        logits = [sb.tile([P, N], F32, name=f"logit{t}") for t in range(2)]
+        rates = [sb.tile([P, N], F32, name=f"rate{t}") for t in range(2)]
+        results = [sb.tile([P, N], F32, name=f"res{t}") for t in range(2)]
+
+        def step(i):
+            t, c0, width = steps[i]
+            score, c = scores[t, c0]
+            cols = slice(c0, c0 + width)
+            b0 = c0 % HALF
+            nc.vector.tensor_tensor(logits[t][:, cols], score[:, c : c + width], bias_all[c0 // HALF][:, b0 : b0 + width], ADD)
+            nc.scalar.activation(rates[t][:, cols], logits[t][:, cols], EXP)
+
+        def finish(i):
+            t, c0, width = stores[i]
+            cols = slice(c0, c0 + width)
+            nc.vector.tensor_scalar(results[t][:, cols], rates[t][:, cols], expo[:, t : t + 1], None, MULT)
+            nc.sync.dma_start(out=out[0, t * P : (t + 1) * P, cols], in_=results[t][:, cols])
+
+        step(0)
+        step(1)
+        step(2)
+        step(3)
+        step(4)
+        step(5)
+        finish(0)
+        step(6)
+        step(7)
+        finish(1)
+        finish(2)
+        finish(3)
+        finish(4)

@@ -15,6 +15,7 @@ U16 = mybir.dt.uint16
 U8 = mybir.dt.uint8
 FP8X4 = mybir.dt.float8_e4m3fn_x4
 EXP = mybir.ActivationFunctionType.Exp
+COPY = mybir.ActivationFunctionType.Copy
 ADD = mybir.AluOpType.add
 MULT = mybir.AluOpType.mult
 
@@ -22,6 +23,8 @@ P = 128
 PACK = 4
 HALF = N // 2
 LIST_COLS = N // 16
+BLOCKS = N // P
+STAGE = 48
 
 
 def tile_attend_rate_topk_kernel(tc, qT, k_words, k_scales, kb, ex, offs, out):
@@ -30,10 +33,10 @@ def tile_attend_rate_topk_kernel(tc, qT, k_words, k_scales, kb, ex, offs, out):
         sb = ctx.enter_context(tc.tile_pool(name="sb", bufs=1))
         ps = ctx.enter_context(tc.psum_pool(name="ps", bufs=1))
 
-        bias_row = sb.tile([P, T], F32, name="bias_row", tag="bias_slot", align_bytes=64)
+        bias_row = sb.tile([P, T], F32, name="bias_row", align_bytes=64)
         nc.scalar.dma_start(out=bias_row[P - 1 : P, :], in_=kb[0:1, :])
         scales = sb.tile([P, T], U8, name="scales", align_bytes=64)
-        nc.sync.dma_start(out=scales[48:64, :].bitcast(I32), in_=k_scales[0].bitcast(I32))
+        nc.sync.dma_start(out=scales[STAGE : STAGE + 16, :].bitcast(I32), in_=k_scales[0].bitcast(I32))
         offsets = sb.tile([P, LIST_COLS], U16, name="offsets")
         nc.sync.dma_start(offsets[:], offs)
 
@@ -42,37 +45,39 @@ def tile_attend_rate_topk_kernel(tc, qT, k_words, k_scales, kb, ex, offs, out):
         words = sb.tile([P, T], I32, name="words", align_bytes=64)
         nc.sync.dma_start(out=words[:], in_=k_words[0].rearrange("p t r -> p (t r)").bitcast(I32))
         expo = sb.tile([P, 2], F32, name="expo")
-        with nc.allow_non_contiguous_dma(reason="one exposure a partition"):
-            nc.sync.dma_start(out=expo[:], in_=ex[0].rearrange("(t p) o -> p (t o)", p=P))
+        nc.sync.dma_start(out=expo[:], in_=ex[0].rearrange("(p t) o -> p (t o)", t=2))
 
-        nc.vector.memset(scales[0:48, :].bitcast(I32), 0)
-        nc.vector.memset(scales[64:P, :].bitcast(I32), 0)
+        seed = sb.tile([P, 1], F32, name="seed")
+        nc.gpsimd.memset(seed[:], 0.0)
+        warm = sb.tile([P, 1], F32, name="warm")
+        nc.scalar.activation(warm[:], seed[:], EXP)
+
+        nc.vector.memset(scales[0:STAGE, :].bitcast(I32), 0)
+        nc.vector.memset(scales[STAGE + 16 : P, :].bitcast(I32), 0)
         ident = sb.tile([P, P], F32, name="ident")
         make_identity(nc, ident[:])
-        k_sc = sb.tile([P, N], U8, name="k_sc", align_bytes=64)
         nc.vector.memset(bias_row[0 : P - 1, :], 0.0)
+
+        def listed(first, count):
+            return offsets[:, first // 16 : (first + count) // 16]
 
         listed_sc = sb.tile([P, N], U8, name="listed_sc", align_bytes=64)
         nc.vector.tensor_copy(listed_sc[:], scales[:].indirect(offsets[:]))
+        k_sc = sb.tile([P, N], U8, name="k_sc", align_bytes=64)
         for quad in range(4):
             nc.sync.dma_start(
                 out=k_sc[32 * quad : 32 * quad + 4, :].bitcast(I32),
-                in_=listed_sc[48 + 4 * quad : 52 + 4 * quad, :].bitcast(I32),
+                in_=listed_sc[STAGE + 4 * quad : STAGE + 4 * quad + 4, :].bitcast(I32),
             )
 
-        def half_list(h):
-            return offsets[:, h * (LIST_COLS // 2) : (h + 1) * (LIST_COLS // 2)]
-
-        q_bf = sb.tile([P, NQ, PACK], BF16, name="q_bf", tag="operand_slot", align_bytes=64)
-        nc.scalar.copy(q_bf[:], q_raw[:].rearrange("p j q -> p q j"))
-
+        bias_listed = [sb.tile([P, HALF], F32, name=f"bias_listed{h}") for h in range(2)]
+        for h in range(2):
+            nc.scalar.activation(bias_listed[h][:], bias_row[:].indirect(listed(h * HALF, HALF)), COPY)
         bias_all = []
         for h in range(2):
-            bias_listed = sb.tile([P, HALF], F32, name=f"bias_listed{h}")
-            nc.vector.tensor_copy(bias_listed[:], bias_row[:].indirect(half_list(h)))
             turned = ps.tile([P, 2, P], F32, name="turned", tag=f"bias_bank{h}")
             for s in range(2):
-                nc.tensor.transpose(turned[:, s, :], bias_listed[:, s * P : (s + 1) * P], ident[:])
+                nc.tensor.transpose(turned[:, s, :], bias_listed[h][:, s * P : (s + 1) * P], ident[:])
             bias_col = sb.tile([P, 2], F32, name=f"bias_col{h}")
             nc.scalar.copy(bias_col[:], turned[:, :, P - 1])
             spread = ps.tile([P, 2, P], F32, name="spread", tag=f"bias_bank{h}")
@@ -82,26 +87,23 @@ def tile_attend_rate_topk_kernel(tc, qT, k_words, k_scales, kb, ex, offs, out):
             nc.scalar.copy(bias_h[:], spread[:].rearrange("p s c -> p (s c)"))
             bias_all.append(bias_h)
 
-        q_codes = sb.tile([P, NQ], U32, name="q_codes", tag="bias_slot", align_bytes=64)
+        q_bf = sb.tile([P, 2, P, PACK], BF16, name="q_bf", tag="operand_slot", align_bytes=64)
+        nc.vector.tensor_copy(q_bf[:], q_raw[:].rearrange("p j (m t) -> p t m j", t=2))
+        q_codes = sb.tile([P, NQ], U32, name="q_codes", align_bytes=64)
         q_sc = sb.tile([P, NQ], U8, name="q_sc", align_bytes=64)
         nc.vector.quantize_mx(
-            out=q_codes[:].bitcast(FP8X4), scales=q_sc[:], in_=q_bf[:].rearrange("p q j -> p (q j)")
+            out=q_codes[:].bitcast(FP8X4), scales=q_sc[:], in_=q_bf[:].rearrange("p t m j -> p (t m j)")
         )
 
         k_codes = sb.tile([P, N], U32, name="k_codes", tag="operand_slot", align_bytes=64)
-        passes = [(0, 0, 128), (0, 128, 128), (1, 0, 128), (1, 128, 128), (0, 256, 128), (0, 384, 128), (1, 256, 128), (1, 384, 128)]
-        steps = [(0, 0, 128), (0, 128, 128), (1, 0, 128), (1, 128, 128), (0, 256, 128), (0, 384, 128), (1, 256, 128), (1, 384, 128)]
-        stores = [(0, 0, 256), (1, 0, 256), (0, 256, 256), (1, 256, 128), (1, 384, 128)]
         scores = {}
-        for h in range(2):
-            nc.vector.tensor_copy(k_codes[:, h * HALF : (h + 1) * HALF], words[:].bitcast(U32).indirect(half_list(h)))
-            for i, (t, c0, width) in enumerate(passes):
-                if c0 // HALF != h:
-                    continue
+        for b in range(BLOCKS):
+            cols = slice(b * P, (b + 1) * P)
+            nc.vector.tensor_copy(k_codes[:, cols], words[:].bitcast(U32).indirect(listed(b * P, P)))
+            for t in range(2):
                 rows = slice(t * P, (t + 1) * P)
-                cols = slice(c0, c0 + width)
-                bank = f"bias_bank{i - 6}" if i >= 6 else f"score{i}"
-                score = ps.tile([P, width], F32, name=f"score{i}", tag=bank)
+                bank = f"bias_bank{t}" if b == BLOCKS - 1 else f"score{b}_{t}"
+                score = ps.tile([P, P], F32, name=f"score{b}_{t}", tag=bank)
                 nc.tensor.matmul_mx(
                     out=score[:],
                     lhsT=q_codes[:, rows].bitcast(FP8X4),
@@ -111,37 +113,35 @@ def tile_attend_rate_topk_kernel(tc, qT, k_words, k_scales, kb, ex, offs, out):
                     start=True,
                     stop=True,
                 )
-                for c in range(0, width, 64):
-                    scores[t, c0 + c] = (score, c)
+                scores[t, b] = score
 
         logits = [sb.tile([P, N], F32, name=f"logit{t}") for t in range(2)]
         rates = [sb.tile([P, N], F32, name=f"rate{t}") for t in range(2)]
         results = [sb.tile([P, N], F32, name=f"res{t}") for t in range(2)]
 
-        def step(i):
-            t, c0, width = steps[i]
-            score, c = scores[t, c0]
-            cols = slice(c0, c0 + width)
-            b0 = c0 % HALF
-            nc.vector.tensor_tensor(logits[t][:, cols], score[:, c : c + width], bias_all[c0 // HALF][:, b0 : b0 + width], ADD)
+        out_rows = out[0].rearrange("(m t) n -> t m n", t=2)
+
+        def rate(t, b):
+            cols = slice(b * P, (b + 1) * P)
+            b0 = (b * P) % HALF
+            nc.vector.tensor_tensor(logits[t][:, cols], scores[t, b][:], bias_all[b * P // HALF][:, b0 : b0 + P], ADD)
             nc.scalar.activation(rates[t][:, cols], logits[t][:, cols], EXP)
 
-        def finish(i):
-            t, c0, width = stores[i]
-            cols = slice(c0, c0 + width)
+        def finish(t, first, count):
+            cols = slice(first * P, (first + count) * P)
             nc.vector.tensor_scalar(results[t][:, cols], rates[t][:, cols], expo[:, t : t + 1], None, MULT)
-            nc.sync.dma_start(out=out[0, t * P : (t + 1) * P, cols], in_=results[t][:, cols])
+            nc.sync.dma_start(out=out_rows[t, :, cols], in_=results[t][:, cols])
 
-        step(0)
-        step(1)
-        step(2)
-        step(3)
-        step(4)
-        step(5)
-        finish(0)
-        step(6)
-        step(7)
-        finish(1)
-        finish(2)
-        finish(3)
-        finish(4)
+        rate(0, 0)
+        rate(0, 1)
+        rate(1, 0)
+        rate(1, 1)
+        rate(0, 2)
+        rate(0, 3)
+        finish(0, 0, 2)
+        rate(1, 2)
+        rate(1, 3)
+        finish(1, 0, 2)
+        finish(0, 2, 2)
+        finish(1, 2, 1)
+        finish(1, 3, 1)

@@ -33,7 +33,7 @@ def tile_attend_rate_topk_kernel(tc, qT, k_words, k_scales, kb, ex, offs, out):
         sb = ctx.enter_context(tc.tile_pool(name="sb", bufs=1))
         ps = ctx.enter_context(tc.psum_pool(name="ps", bufs=1))
 
-        bias_row = sb.tile([P, T], F32, name="bias_row", align_bytes=64)
+        bias_row = sb.tile([P, T], F32, name="bias_row", tag="bias_slot", align_bytes=64)
         nc.scalar.dma_start(out=bias_row[P - 1 : P, :], in_=kb[0:1, :])
         scales = sb.tile([P, T], U8, name="scales", align_bytes=64)
         nc.sync.dma_start(out=scales[STAGE : STAGE + 16, :].bitcast(I32), in_=k_scales[0].bitcast(I32))
@@ -63,16 +63,16 @@ def tile_attend_rate_topk_kernel(tc, qT, k_words, k_scales, kb, ex, offs, out):
 
         listed_sc = sb.tile([P, N], U8, name="listed_sc", align_bytes=64)
         nc.vector.tensor_copy(listed_sc[:], scales[:].indirect(offsets[:]))
-        k_sc = sb.tile([P, N], U8, name="k_sc", align_bytes=64)
-        for quad in range(4):
-            nc.sync.dma_start(
-                out=k_sc[32 * quad : 32 * quad + 4, :].bitcast(I32),
-                in_=listed_sc[STAGE + 4 * quad : STAGE + 4 * quad + 4, :].bitcast(I32),
-            )
 
         bias_listed = [sb.tile([P, HALF], F32, name=f"bias_listed{h}") for h in range(2)]
         for h in range(2):
             nc.scalar.activation(bias_listed[h][:], bias_row[:].indirect(listed(h * HALF, HALF)), COPY)
+        k_sc = sb.tile([P, N], U8, name="k_sc", tag="bias_slot", align_bytes=64)
+        for quad in range(4):
+            nc.scalar.dma_start(
+                out=k_sc[32 * quad : 32 * quad + 4, :].bitcast(I32),
+                in_=listed_sc[STAGE + 4 * quad : STAGE + 4 * quad + 4, :].bitcast(I32),
+            )
         bias_all = []
         for h in range(2):
             turned = ps.tile([P, 2, P], F32, name="turned", tag=f"bias_bank{h}")

@@ -52,11 +52,11 @@ def tile_attend_rate_topk_kernel(tc, qT, k_words, k_scales, kb, ex, offs, out):
         warm = sb.tile([P, 1], F32, name="warm")
         nc.scalar.activation(warm[:], seed[:], EXP)
 
+        nc.vector.memset(bias_row[0 : P - 1, :], 0.0)
         nc.vector.memset(scales[0:STAGE, :].bitcast(I32), 0)
         nc.vector.memset(scales[STAGE + 16 : P, :].bitcast(I32), 0)
         ident = sb.tile([P, P], F32, name="ident")
         make_identity(nc, ident[:])
-        nc.vector.memset(bias_row[0 : P - 1, :], 0.0)
 
         def listed(first, count):
             return offsets[:, first // 16 : (first + count) // 16]

@@ -40,21 +40,25 @@ def tile_attend_rate_topk_kernel(tc, qT, k_words, k_scales, kb, ex, offs, out):
         offsets = sb.tile([P, LIST_COLS], U16, name="offsets")
         nc.sync.dma_start(offsets[:], offs)
 
-        q_raw = sb.tile([P, PACK, NQ], F32, name="q_raw")
-        nc.sync.dma_start(out=q_raw[:], in_=qT[0].rearrange("(p j) q -> p j q", j=PACK))
+        q_rows = qT[0].rearrange("(p j) q -> p j q", j=PACK)
+        q_raw0 = sb.tile([P, PACK, P], F32, name="q_raw0")
+        nc.sync.dma_start(out=q_raw0[:], in_=q_rows[:, :, 0:P])
         words = sb.tile([P, T], I32, name="words", align_bytes=64)
         nc.sync.dma_start(out=words[:], in_=k_words[0].rearrange("p t r -> p (t r)").bitcast(I32))
+        q_raw1 = sb.tile([P, PACK, P], F32, name="q_raw1", tag="late_slot")
+        nc.sync.dma_start(out=q_raw1[:], in_=q_rows[:, :, P:NQ])
         expo = sb.tile([P, 2], F32, name="expo")
-        nc.sync.dma_start(out=expo[:], in_=ex[0].rearrange("(p t) o -> p (t o)", t=2))
+        with nc.allow_non_contiguous_dma(reason="one exposure a partition and query tile"):
+            nc.sync.dma_start(out=expo[:], in_=ex[0].rearrange("(t p) o -> p (t o)", t=2))
 
         seed = sb.tile([P, 1], F32, name="seed")
         nc.gpsimd.memset(seed[:], 0.0)
         warm = sb.tile([P, 1], F32, name="warm")
         nc.scalar.activation(warm[:], seed[:], EXP)
 
-        nc.vector.memset(bias_row[0 : P - 1, :], 0.0)
         nc.vector.memset(scales[0:STAGE, :].bitcast(I32), 0)
         nc.vector.memset(scales[STAGE + 16 : P, :].bitcast(I32), 0)
+        nc.vector.memset(bias_row[0 : P - 1, :], 0.0)
         ident = sb.tile([P, P], F32, name="ident")
         make_identity(nc, ident[:])
 
@@ -73,53 +77,73 @@ def tile_attend_rate_topk_kernel(tc, qT, k_words, k_scales, kb, ex, offs, out):
                 out=k_sc[32 * quad : 32 * quad + 4, :].bitcast(I32),
                 in_=listed_sc[STAGE + 4 * quad : STAGE + 4 * quad + 4, :].bitcast(I32),
             )
-        bias_all = []
+        bias_all = [sb.tile([P, HALF], F32, name=f"bias_all{h}") for h in range(2)]
+        spreads = []
         for h in range(2):
             turned = ps.tile([P, 2, P], F32, name="turned", tag=f"bias_bank{h}")
             for s in range(2):
                 nc.tensor.transpose(turned[:, s, :], bias_listed[h][:, s * P : (s + 1) * P], ident[:])
-            bias_col = sb.tile([P, 2], F32, name=f"bias_col{h}")
+            bias_col = sb.tile([P, 2], F32, name=f"bias_col{h}", tag=f"col_slot{h}", align_bytes=64)
             nc.scalar.copy(bias_col[:], turned[:, :, P - 1])
             spread = ps.tile([P, 2, P], F32, name="spread", tag=f"bias_bank{h}")
             for s in range(2):
                 nc.tensor.transpose(spread[:, s, :], bias_col[:, s : s + 1].to_broadcast([P, P]), ident[:])
-            bias_h = sb.tile([P, HALF], F32, name=f"bias_all{h}")
-            nc.scalar.copy(bias_h[:], spread[:].rearrange("p s c -> p (s c)"))
-            bias_all.append(bias_h)
+            spreads.append(spread)
 
-        q_bf = sb.tile([P, 2, P, PACK], BF16, name="q_bf", tag="operand_slot", align_bytes=64)
-        nc.vector.tensor_copy(q_bf[:], q_raw[:].rearrange("p j (m t) -> p t m j", t=2))
-        q_codes = sb.tile([P, NQ], U32, name="q_codes", align_bytes=64)
-        q_sc = sb.tile([P, NQ], U8, name="q_sc", align_bytes=64)
-        nc.vector.quantize_mx(
-            out=q_codes[:].bitcast(FP8X4), scales=q_sc[:], in_=q_bf[:].rearrange("p t m j -> p (t m j)")
-        )
+        def fetch_bias(h):
+            nc.scalar.copy(bias_all[h][:], spreads[h][:].rearrange("p s c -> p (s c)"))
+
+        q_codes = [sb.tile([P, P], U32, name=f"q_codes{t}", align_bytes=64) for t in range(2)]
+        q_sc = [sb.tile([P, P], U8, name=f"q_sc{t}", align_bytes=64) for t in range(2)]
+
+        def quantise(t, rounded):
+            nc.vector.quantize_mx(
+                out=q_codes[t][:].bitcast(FP8X4), scales=q_sc[t][:], in_=rounded[:].rearrange("p m j -> p (m j)")
+            )
+
+        def by_fours(rounded, raw):
+            return (
+                rounded[:].rearrange("p (c i) j -> p c j i", i=4),
+                raw[:].rearrange("p j (c i) -> p c j i", i=4),
+            )
+
+        q_bf0 = sb.tile([P, P, PACK], BF16, name="q_bf0", tag="operand_slot", align_bytes=64)
+        nc.vector.tensor_copy(*by_fours(q_bf0, q_raw0))
+        quantise(0, q_bf0)
+        fetch_bias(0)
+        q_bf1 = sb.tile([P, P, PACK], BF16, name="q_bf1", tag="col_slot0", align_bytes=64)
+        nc.scalar.copy(*by_fours(q_bf1, q_raw1))
+        fetch_bias(1)
 
         k_codes = sb.tile([P, N], U32, name="k_codes", tag="operand_slot", align_bytes=64)
         scores = {}
+
+        def score(t, b):
+            cols = slice(b * P, (b + 1) * P)
+            bank = f"bias_bank{b - 2}" if t == 1 and b >= 2 else f"score{t}_{b}"
+            tile = ps.tile([P, P], F32, name=f"score{t}_{b}", tag=bank)
+            nc.tensor.matmul_mx(
+                out=tile[:],
+                lhsT=q_codes[t][:].bitcast(FP8X4),
+                lhsT_scale=q_sc[t][:],
+                rhs=k_codes[:, cols].bitcast(FP8X4),
+                rhs_scale=k_sc[:, cols],
+                start=True,
+                stop=True,
+            )
+            scores[t, b] = tile
+
         for b in range(BLOCKS):
             cols = slice(b * P, (b + 1) * P)
             nc.vector.tensor_copy(k_codes[:, cols], words[:].bitcast(U32).indirect(listed(b * P, P)))
-            for t in range(2):
-                rows = slice(t * P, (t + 1) * P)
-                bank = f"bias_bank{t}" if b == BLOCKS - 1 else f"score{b}_{t}"
-                score = ps.tile([P, P], F32, name=f"score{b}_{t}", tag=bank)
-                nc.tensor.matmul_mx(
-                    out=score[:],
-                    lhsT=q_codes[:, rows].bitcast(FP8X4),
-                    lhsT_scale=q_sc[:, rows],
-                    rhs=k_codes[:, cols].bitcast(FP8X4),
-                    rhs_scale=k_sc[:, cols],
-                    start=True,
-                    stop=True,
-                )
-                scores[t, b] = score
+            score(0, b)
 
-        logits = [sb.tile([P, N], F32, name=f"logit{t}") for t in range(2)]
+        logits = [
+            sb.tile([P, N], F32, name="logit0", tag="late_slot"),
+            sb.tile([P, N], F32, name="logit1"),
+        ]
         rates = [sb.tile([P, N], F32, name=f"rate{t}") for t in range(2)]
         results = [sb.tile([P, N], F32, name=f"res{t}") for t in range(2)]
-
-        out_rows = out[0].rearrange("(m t) n -> t m n", t=2)
 
         def rate(t, b):
             cols = slice(b * P, (b + 1) * P)
@@ -130,18 +154,21 @@ def tile_attend_rate_topk_kernel(tc, qT, k_words, k_scales, kb, ex, offs, out):
         def finish(t, first, count):
             cols = slice(first * P, (first + count) * P)
             nc.vector.tensor_scalar(results[t][:, cols], rates[t][:, cols], expo[:, t : t + 1], None, MULT)
-            nc.sync.dma_start(out=out_rows[t, :, cols], in_=results[t][:, cols])
+            nc.sync.dma_start(out=out[0, t * P : (t + 1) * P, cols], in_=results[t][:, cols])
 
+        quantise(1, q_bf1)
+        for b in range(BLOCKS):
+            score(1, b)
         rate(0, 0)
         rate(0, 1)
-        rate(1, 0)
-        rate(1, 1)
         rate(0, 2)
         rate(0, 3)
         finish(0, 0, 2)
+        rate(1, 0)
+        rate(1, 1)
+        finish(0, 2, 2)
         rate(1, 2)
         rate(1, 3)
         finish(1, 0, 2)
-        finish(0, 2, 2)
         finish(1, 2, 1)
         finish(1, 3, 1)

@@ -33,7 +33,7 @@ def tile_attend_rate_topk_kernel(tc, qT, k_words, k_scales, kb, ex, offs, out):
         sb = ctx.enter_context(tc.tile_pool(name="sb", bufs=1))
         ps = ctx.enter_context(tc.psum_pool(name="ps", bufs=1))
 
-        bias_row = sb.tile([P, T], F32, name="bias_row", tag="bias_slot", align_bytes=64)
+        bias_row = sb.tile([P, T], F32, name="bias_row", align_bytes=64)
         nc.scalar.dma_start(out=bias_row[P - 1 : P, :], in_=kb[0:1, :])
         scales = sb.tile([P, T], U8, name="scales", align_bytes=64)
         nc.sync.dma_start(out=scales[STAGE : STAGE + 16, :].bitcast(I32), in_=k_scales[0].bitcast(I32))
@@ -56,9 +56,9 @@ def tile_attend_rate_topk_kernel(tc, qT, k_words, k_scales, kb, ex, offs, out):
         warm = sb.tile([P, 1], F32, name="warm")
         nc.scalar.activation(warm[:], seed[:], EXP)
 
+        nc.vector.memset(bias_row[0 : P - 1, :], 0.0)
         nc.vector.memset(scales[0:STAGE, :].bitcast(I32), 0)
         nc.vector.memset(scales[STAGE + 16 : P, :].bitcast(I32), 0)
-        nc.vector.memset(bias_row[0 : P - 1, :], 0.0)
         ident = sb.tile([P, P], F32, name="ident")
         make_identity(nc, ident[:])
 
@@ -71,9 +71,9 @@ def tile_attend_rate_topk_kernel(tc, qT, k_words, k_scales, kb, ex, offs, out):
         bias_listed = [sb.tile([P, HALF], F32, name=f"bias_listed{h}") for h in range(2)]
         for h in range(2):
             nc.scalar.activation(bias_listed[h][:], bias_row[:].indirect(listed(h * HALF, HALF)), COPY)
-        k_sc = sb.tile([P, N], U8, name="k_sc", tag="bias_slot", align_bytes=64)
+        k_sc = sb.tile([P, N], U8, name="k_sc", align_bytes=64)
         for quad in range(4):
-            nc.scalar.dma_start(
+            nc.sync.dma_start(
                 out=k_sc[32 * quad : 32 * quad + 4, :].bitcast(I32),
                 in_=listed_sc[STAGE + 4 * quad : STAGE + 4 * quad + 4, :].bitcast(I32),
             )

@@ -1,7 +1,6 @@
 from contextlib import ExitStack
 
 import concourse.mybir as mybir
-from concourse.masks import make_identity
 
 D, NQ, T, N = 512, 256, 2048, 512
 FLOPS = 2 * D * NQ * N
@@ -35,140 +34,128 @@ def tile_attend_rate_topk_kernel(tc, qT, k_words, k_scales, kb, ex, offs, out):
 
         bias_row = sb.tile([P, T], F32, name="bias_row", align_bytes=64)
         nc.scalar.dma_start(out=bias_row[P - 1 : P, :], in_=kb[0:1, :])
+        expo_rows = sb.tile([P, P], F32, name="expo_rows")
+        nc.scalar.dma_start(out=expo_rows[P - 2 : P, :], in_=ex[0].rearrange("(t p) o -> t (p o)", t=2))
         scales = sb.tile([P, T], U8, name="scales", align_bytes=64)
         nc.sync.dma_start(out=scales[STAGE : STAGE + 16, :].bitcast(I32), in_=k_scales[0].bitcast(I32))
         offsets = sb.tile([P, LIST_COLS], U16, name="offsets")
         nc.sync.dma_start(offsets[:], offs)
-
-        q_rows = qT[0].rearrange("(p j) q -> p j q", j=PACK)
-        q_raw0 = sb.tile([P, PACK, P], F32, name="q_raw0")
-        nc.sync.dma_start(out=q_raw0[:], in_=q_rows[:, :, 0:P])
+        q_raw = sb.tile([P, PACK, NQ], F32, name="q_raw")
+        nc.sync.dma_start(out=q_raw[:], in_=qT[0].rearrange("(p j) q -> p j q", j=PACK))
         words = sb.tile([P, T], I32, name="words", align_bytes=64)
         nc.sync.dma_start(out=words[:], in_=k_words[0].rearrange("p t r -> p (t r)").bitcast(I32))
-        q_raw1 = sb.tile([P, PACK, P], F32, name="q_raw1", tag="late_slot")
-        nc.sync.dma_start(out=q_raw1[:], in_=q_rows[:, :, P:NQ])
-        expo = sb.tile([P, 2], F32, name="expo")
-        with nc.allow_non_contiguous_dma(reason="one exposure a partition and query tile"):
-            nc.sync.dma_start(out=expo[:], in_=ex[0].rearrange("(t p) o -> p (t o)", t=2))
 
         seed = sb.tile([P, 1], F32, name="seed")
         nc.gpsimd.memset(seed[:], 0.0)
         warm = sb.tile([P, 1], F32, name="warm")
         nc.scalar.activation(warm[:], seed[:], EXP)
 
-        nc.vector.memset(bias_row[0 : P - 1, :], 0.0)
+        nc.gpsimd.memset(scales[STAGE + 16 : P, :].bitcast(I32), 0)
         nc.vector.memset(scales[0:STAGE, :].bitcast(I32), 0)
-        nc.vector.memset(scales[STAGE + 16 : P, :].bitcast(I32), 0)
+        nc.vector.memset(bias_row[0 : P - 1, :], 0.0)
+        nc.vector.memset(expo_rows[0 : P - 2, :], 0.0)
         ident = sb.tile([P, P], F32, name="ident")
-        make_identity(nc, ident[:])
+        nc.vector.memset(ident[:], 0.0)
+        nc.gpsimd.affine_select(
+            out=ident[:],
+            in_=ident[:],
+            compare_op=mybir.AluOpType.not_equal,
+            fill=1.0,
+            base=0,
+            pattern=[[-1, P]],
+            channel_multiplier=1,
+        )
 
         def listed(first, count):
             return offsets[:, first // 16 : (first + count) // 16]
 
         listed_sc = sb.tile([P, N], U8, name="listed_sc", align_bytes=64)
         nc.vector.tensor_copy(listed_sc[:], scales[:].indirect(offsets[:]))
-
-        bias_listed = [sb.tile([P, HALF], F32, name=f"bias_listed{h}") for h in range(2)]
-        for h in range(2):
-            nc.scalar.activation(bias_listed[h][:], bias_row[:].indirect(listed(h * HALF, HALF)), COPY)
         k_sc = sb.tile([P, N], U8, name="k_sc", align_bytes=64)
         for quad in range(4):
             nc.sync.dma_start(
                 out=k_sc[32 * quad : 32 * quad + 4, :].bitcast(I32),
                 in_=listed_sc[STAGE + 4 * quad : STAGE + 4 * quad + 4, :].bitcast(I32),
             )
+
+        expo_turned = ps.tile([P, P], F32, name="expo_turned", tag="score0_0")
+        nc.tensor.transpose(expo_turned[:], expo_rows[:], ident[:])
+        bias_listed = [sb.tile([P, HALF], F32, name=f"bias_listed{h}", tag=f"listed_slot{h}", align_bytes=64) for h in range(2)]
+        nc.scalar.activation(bias_listed[0][:], bias_row[:].indirect(listed(0, HALF)), COPY)
+        nc.vector.tensor_copy(bias_listed[1][:], bias_row[:].indirect(listed(HALF, HALF)))
         bias_all = [sb.tile([P, HALF], F32, name=f"bias_all{h}") for h in range(2)]
         spreads = []
         for h in range(2):
             turned = ps.tile([P, 2, P], F32, name="turned", tag=f"bias_bank{h}")
             for s in range(2):
                 nc.tensor.transpose(turned[:, s, :], bias_listed[h][:, s * P : (s + 1) * P], ident[:])
-            bias_col = sb.tile([P, 2], F32, name=f"bias_col{h}", tag=f"col_slot{h}", align_bytes=64)
+            bias_col = sb.tile([P, 2], F32, name=f"bias_col{h}")
             nc.scalar.copy(bias_col[:], turned[:, :, P - 1])
             spread = ps.tile([P, 2, P], F32, name="spread", tag=f"bias_bank{h}")
             for s in range(2):
                 nc.tensor.transpose(spread[:, s, :], bias_col[:, s : s + 1].to_broadcast([P, P]), ident[:])
             spreads.append(spread)
-
-        def fetch_bias(h):
+        for h in range(2):
             nc.scalar.copy(bias_all[h][:], spreads[h][:].rearrange("p s c -> p (s c)"))
 
-        q_codes = [sb.tile([P, P], U32, name=f"q_codes{t}", align_bytes=64) for t in range(2)]
-        q_sc = [sb.tile([P, P], U8, name=f"q_sc{t}", align_bytes=64) for t in range(2)]
+        expo = sb.tile([P, 2], F32, name="expo")
+        nc.scalar.copy(expo[:], expo_turned[:, P - 2 : P])
 
-        def quantise(t, rounded):
-            nc.vector.quantize_mx(
-                out=q_codes[t][:].bitcast(FP8X4), scales=q_sc[t][:], in_=rounded[:].rearrange("p m j -> p (m j)")
-            )
-
-        def by_fours(rounded, raw):
-            return (
-                rounded[:].rearrange("p (c i) j -> p c j i", i=4),
-                raw[:].rearrange("p j (c i) -> p c j i", i=4),
-            )
-
-        q_bf0 = sb.tile([P, P, PACK], BF16, name="q_bf0", tag="operand_slot", align_bytes=64)
-        nc.vector.tensor_copy(*by_fours(q_bf0, q_raw0))
-        quantise(0, q_bf0)
-        fetch_bias(0)
-        q_bf1 = sb.tile([P, P, PACK], BF16, name="q_bf1", tag="col_slot0", align_bytes=64)
-        nc.scalar.copy(*by_fours(q_bf1, q_raw1))
-        fetch_bias(1)
+        q_bf = sb.tile([P, NQ, PACK], BF16, name="q_bf", tag="operand_slot", align_bytes=64)
+        nc.vector.tensor_copy(
+            q_bf[:].rearrange("p (c i) j -> p c j i", i=4), q_raw[:].rearrange("p j (c i) -> p c j i", i=4)
+        )
+        q_codes = sb.tile([P, NQ], U32, name="q_codes", tag="listed_slot1", align_bytes=64)
+        q_sc = sb.tile([P, NQ], U8, name="q_sc", align_bytes=64)
+        nc.vector.quantize_mx(
+            out=q_codes[:].bitcast(FP8X4), scales=q_sc[:], in_=q_bf[:].rearrange("p m j -> p (m j)")
+        )
 
         k_codes = sb.tile([P, N], U32, name="k_codes", tag="operand_slot", align_bytes=64)
         scores = {}
-
-        def score(t, b):
-            cols = slice(b * P, (b + 1) * P)
-            bank = f"bias_bank{b - 2}" if t == 1 and b >= 2 else f"score{t}_{b}"
-            tile = ps.tile([P, P], F32, name=f"score{t}_{b}", tag=bank)
-            nc.tensor.matmul_mx(
-                out=tile[:],
-                lhsT=q_codes[t][:].bitcast(FP8X4),
-                lhsT_scale=q_sc[t][:],
-                rhs=k_codes[:, cols].bitcast(FP8X4),
-                rhs_scale=k_sc[:, cols],
-                start=True,
-                stop=True,
-            )
-            scores[t, b] = tile
-
         for b in range(BLOCKS):
-            cols = slice(b * P, (b + 1) * P)
-            nc.vector.tensor_copy(k_codes[:, cols], words[:].bitcast(U32).indirect(listed(b * P, P)))
-            score(0, b)
+            keys = k_codes[:, b * P : (b + 1) * P]
+            nc.vector.tensor_copy(keys, words[:].bitcast(U32).indirect(listed(b * P, P)))
+            for t in range(2):
+                bank = f"bias_bank{t}" if b == BLOCKS - 1 else f"score{t}_{b}"
+                tile = ps.tile([P, P], F32, name=f"score{t}_{b}", tag=bank)
+                nc.tensor.matmul_mx(
+                    out=tile[:],
+                    lhsT=q_codes[:, t * P : (t + 1) * P].bitcast(FP8X4),
+                    lhsT_scale=q_sc[:, t * P : (t + 1) * P],
+                    rhs=keys.bitcast(FP8X4),
+                    rhs_scale=k_sc[:, b * P : (b + 1) * P],
+                    start=True,
+                    stop=True,
+                )
+                scores[t, b] = tile
 
-        logits = [
-            sb.tile([P, N], F32, name="logit0", tag="late_slot"),
-            sb.tile([P, N], F32, name="logit1"),
-        ]
         rates = [sb.tile([P, N], F32, name=f"rate{t}") for t in range(2)]
         results = [sb.tile([P, N], F32, name=f"res{t}") for t in range(2)]
 
         def rate(t, b):
             cols = slice(b * P, (b + 1) * P)
             b0 = (b * P) % HALF
-            nc.vector.tensor_tensor(logits[t][:, cols], scores[t, b][:], bias_all[b * P // HALF][:, b0 : b0 + P], ADD)
-            nc.scalar.activation(rates[t][:, cols], logits[t][:, cols], EXP)
+            slot = (1, 1) if (t, b) == (1, BLOCKS - 1) else (t, b)
+            logit = sb.tile([P, P], F32, name="logit", tag=f"logit{slot[0]}_{slot[1]}")
+            nc.vector.tensor_tensor(logit[:], scores[t, b][:], bias_all[b * P // HALF][:, b0 : b0 + P], ADD)
+            nc.scalar.activation(rates[t][:, cols], logit[:], EXP)
 
         def finish(t, first, count):
             cols = slice(first * P, (first + count) * P)
             nc.vector.tensor_scalar(results[t][:, cols], rates[t][:, cols], expo[:, t : t + 1], None, MULT)
             nc.sync.dma_start(out=out[0, t * P : (t + 1) * P, cols], in_=results[t][:, cols])
 
-        quantise(1, q_bf1)
-        for b in range(BLOCKS):
-            score(1, b)
         rate(0, 0)
         rate(0, 1)
-        rate(0, 2)
-        rate(0, 3)
-        finish(0, 0, 2)
         rate(1, 0)
         rate(1, 1)
-        finish(0, 2, 2)
+        rate(0, 2)
         rate(1, 2)
+        finish(0, 0, 2)
+        rate(0, 3)
         rate(1, 3)
         finish(1, 0, 2)
         finish(1, 2, 1)
+        finish(0, 2, 2)
         finish(1, 3, 1)

@@ -1,6 +1,7 @@
 from contextlib import ExitStack
 
 import concourse.mybir as mybir
+from concourse.masks import make_identity
 
 D, NQ, T, N = 512, 256, 2048, 512
 FLOPS = 2 * D * NQ * N
@@ -50,21 +51,12 @@ def tile_attend_rate_topk_kernel(tc, qT, k_words, k_scales, kb, ex, offs, out):
         warm = sb.tile([P, 1], F32, name="warm")
         nc.scalar.activation(warm[:], seed[:], EXP)
 
-        nc.gpsimd.memset(scales[STAGE + 16 : P, :].bitcast(I32), 0)
+        nc.vector.memset(scales[STAGE + 16 : P, :].bitcast(I32), 0)
         nc.vector.memset(scales[0:STAGE, :].bitcast(I32), 0)
         nc.vector.memset(bias_row[0 : P - 1, :], 0.0)
         nc.vector.memset(expo_rows[0 : P - 2, :], 0.0)
         ident = sb.tile([P, P], F32, name="ident")
-        nc.vector.memset(ident[:], 0.0)
-        nc.gpsimd.affine_select(
-            out=ident[:],
-            in_=ident[:],
-            compare_op=mybir.AluOpType.not_equal,
-            fill=1.0,
-            base=0,
-            pattern=[[-1, P]],
-            channel_multiplier=1,
-        )
+        make_identity(nc, ident[:])
 
         def listed(first, count):
             return offsets[:, first // 16 : (first + count) // 16]
@@ -81,8 +73,8 @@ def tile_attend_rate_topk_kernel(tc, qT, k_words, k_scales, kb, ex, offs, out):
         expo_turned = ps.tile([P, P], F32, name="expo_turned", tag="score0_0")
         nc.tensor.transpose(expo_turned[:], expo_rows[:], ident[:])
         bias_listed = [sb.tile([P, HALF], F32, name=f"bias_listed{h}", tag=f"listed_slot{h}", align_bytes=64) for h in range(2)]
-        nc.scalar.activation(bias_listed[0][:], bias_row[:].indirect(listed(0, HALF)), COPY)
-        nc.vector.tensor_copy(bias_listed[1][:], bias_row[:].indirect(listed(HALF, HALF)))
+        for h in range(2):
+            nc.scalar.activation(bias_listed[h][:], bias_row[:].indirect(listed(h * HALF, HALF)), COPY)
         bias_all = [sb.tile([P, HALF], F32, name=f"bias_all{h}") for h in range(2)]
         spreads = []
         for h in range(2):
@@ -105,7 +97,7 @@ def tile_attend_rate_topk_kernel(tc, qT, k_words, k_scales, kb, ex, offs, out):
         nc.vector.tensor_copy(
             q_bf[:].rearrange("p (c i) j -> p c j i", i=4), q_raw[:].rearrange("p j (c i) -> p c j i", i=4)
         )
-        q_codes = sb.tile([P, NQ], U32, name="q_codes", tag="listed_slot1", align_bytes=64)
+        q_codes = sb.tile([P, NQ], U32, name="q_codes", tag="listed_slot0", align_bytes=64)
         q_sc = sb.tile([P, NQ], U8, name="q_sc", align_bytes=64)
         nc.vector.quantize_mx(
             out=q_codes[:].bitcast(FP8X4), scales=q_sc[:], in_=q_bf[:].rearrange("p m j -> p (m j)")

@@ -105,22 +105,29 @@ def tile_attend_rate_topk_kernel(tc, qT, k_words, k_scales, kb, ex, offs, out):
 
         k_codes = sb.tile([P, N], U32, name="k_codes", tag="operand_slot", align_bytes=64)
         scores = {}
+
+        def score(t, b, bank):
+            cols = slice(b * P, (b + 1) * P)
+            tile = ps.tile([P, P], F32, name=f"score{t}_{b}", tag=bank)
+            nc.tensor.matmul_mx(
+                out=tile[:],
+                lhsT=q_codes[:, t * P : (t + 1) * P].bitcast(FP8X4),
+                lhsT_scale=q_sc[:, t * P : (t + 1) * P],
+                rhs=k_codes[:, cols].bitcast(FP8X4),
+                rhs_scale=k_sc[:, cols],
+                start=True,
+                stop=True,
+            )
+            scores[t, b] = tile
+
         for b in range(BLOCKS):
-            keys = k_codes[:, b * P : (b + 1) * P]
-            nc.vector.tensor_copy(keys, words[:].bitcast(U32).indirect(listed(b * P, P)))
+            nc.vector.tensor_copy(
+                k_codes[:, b * P : (b + 1) * P], words[:].bitcast(U32).indirect(listed(b * P, P))
+            )
+        for b in range(BLOCKS - 1):
             for t in range(2):
-                bank = f"bias_bank{t}" if b == BLOCKS - 1 else f"score{t}_{b}"
-                tile = ps.tile([P, P], F32, name=f"score{t}_{b}", tag=bank)
-                nc.tensor.matmul_mx(
-                    out=tile[:],
-                    lhsT=q_codes[:, t * P : (t + 1) * P].bitcast(FP8X4),
-                    lhsT_scale=q_sc[:, t * P : (t + 1) * P],
-                    rhs=keys.bitcast(FP8X4),
-                    rhs_scale=k_sc[:, b * P : (b + 1) * P],
-                    start=True,
-                    stop=True,
-                )
-                scores[t, b] = tile
+                score(t, b, f"score{t}_{b}")
+        score(0, 3, "bias_bank0")
 
         rates = [sb.tile([P, N], F32, name=f"rate{t}") for t in range(2)]
         results = [sb.tile([P, N], F32, name=f"res{t}") for t in range(2)]
@@ -128,8 +135,7 @@ def tile_attend_rate_topk_kernel(tc, qT, k_words, k_scales, kb, ex, offs, out):
         def rate(t, b):
             cols = slice(b * P, (b + 1) * P)
             b0 = (b * P) % HALF
-            slot = (1, 1) if (t, b) == (1, BLOCKS - 1) else (t, b)
-            logit = sb.tile([P, P], F32, name="logit", tag=f"logit{slot[0]}_{slot[1]}")
+            logit = sb.tile([P, P], F32, name=f"logit{t}_{b}")
             nc.vector.tensor_tensor(logit[:], scores[t, b][:], bias_all[b * P // HALF][:, b0 : b0 + P], ADD)
             nc.scalar.activation(rates[t][:, cols], logit[:], EXP)
 
@@ -140,6 +146,7 @@ def tile_attend_rate_topk_kernel(tc, qT, k_words, k_scales, kb, ex, offs, out):
 
         rate(0, 0)
         rate(0, 1)
+        score(1, 3, "score0_1")
         rate(1, 0)
         rate(1, 1)
         rate(0, 2)

@@ -51,7 +51,7 @@ def tile_attend_rate_topk_kernel(tc, qT, k_words, k_scales, kb, ex, offs, out):
         warm = sb.tile([P, 1], F32, name="warm")
         nc.scalar.activation(warm[:], seed[:], EXP)
 
-        nc.vector.memset(scales[STAGE + 16 : P, :].bitcast(I32), 0)
+        nc.gpsimd.memset(scales[STAGE + 16 : P, :].bitcast(I32), 0)
         nc.vector.memset(scales[0:STAGE, :].bitcast(I32), 0)
         nc.vector.memset(bias_row[0 : P - 1, :], 0.0)
         nc.vector.memset(expo_rows[0 : P - 2, :], 0.0)

@@ -37,10 +37,10 @@ def tile_attend_rate_topk_kernel(tc, qT, k_words, k_scales, kb, ex, offs, out):
         nc.scalar.dma_start(out=bias_row[P - 1 : P, :], in_=kb[0:1, :])
         expo_rows = sb.tile([P, P], F32, name="expo_rows")
         nc.scalar.dma_start(out=expo_rows[P - 2 : P, :], in_=ex[0].rearrange("(t p) o -> t (p o)", t=2))
-        scales = sb.tile([P, T], U8, name="scales", align_bytes=64)
-        nc.sync.dma_start(out=scales[STAGE : STAGE + 16, :].bitcast(I32), in_=k_scales[0].bitcast(I32))
         offsets = sb.tile([P, LIST_COLS], U16, name="offsets")
         nc.sync.dma_start(offsets[:], offs)
+        scales = sb.tile([P, T], U8, name="scales", align_bytes=64)
+        nc.sync.dma_start(out=scales[STAGE : STAGE + 16, :].bitcast(I32), in_=k_scales[0].bitcast(I32))
         q_raw = sb.tile([P, PACK, NQ], F32, name="q_raw")
         nc.sync.dma_start(out=q_raw[:], in_=qT[0].rearrange("(p j) q -> p j q", j=PACK))
         words = sb.tile([P, T], I32, name="words", align_bytes=64)

from contextlib import ExitStack

import concourse.mybir as mybir
from concourse.masks import make_identity

D, NQ, T, N = 512, 256, 2048, 512
FLOPS = 2 * D * NQ * N
BYTES = 4 * D * NQ + D * T + (D // 32) * T + 4 * T + 4 * NQ + 2 * 128 * (N // 16) + 4 * NQ * N

F32 = mybir.dt.float32
BF16 = mybir.dt.bfloat16
I32 = mybir.dt.int32
U32 = mybir.dt.uint32
U16 = mybir.dt.uint16
U8 = mybir.dt.uint8
FP8X4 = mybir.dt.float8_e4m3fn_x4
EXP = mybir.ActivationFunctionType.Exp
COPY = mybir.ActivationFunctionType.Copy
ADD = mybir.AluOpType.add
MULT = mybir.AluOpType.mult

P = 128
PACK = 4
HALF = N // 2
LIST_COLS = N // 16
BLOCKS = N // P
STAGE = 48


def tile_attend_rate_topk_kernel(tc, qT, k_words, k_scales, kb, ex, offs, out):
    nc = tc.nc
    with ExitStack() as ctx:
        sb = ctx.enter_context(tc.tile_pool(name="sb", bufs=1))
        ps = ctx.enter_context(tc.psum_pool(name="ps", bufs=1))

        bias_row = sb.tile([P, T], F32, name="bias_row", align_bytes=64)
        nc.scalar.dma_start(out=bias_row[P - 1 : P, :], in_=kb[0:1, :])
        expo_rows = sb.tile([P, P], F32, name="expo_rows")
        nc.scalar.dma_start(out=expo_rows[P - 2 : P, :], in_=ex[0].rearrange("(t p) o -> t (p o)", t=2))
        offsets = sb.tile([P, LIST_COLS], U16, name="offsets")
        nc.sync.dma_start(offsets[:], offs)
        scales = sb.tile([P, T], U8, name="scales", align_bytes=64)
        nc.sync.dma_start(out=scales[STAGE : STAGE + 16, :].bitcast(I32), in_=k_scales[0].bitcast(I32))
        q_raw = sb.tile([P, PACK, NQ], F32, name="q_raw")
        nc.sync.dma_start(out=q_raw[:], in_=qT[0].rearrange("(p j) q -> p j q", j=PACK))
        words = sb.tile([P, T], I32, name="words", align_bytes=64)
        nc.sync.dma_start(out=words[:], in_=k_words[0].rearrange("p t r -> p (t r)").bitcast(I32))

        seed = sb.tile([P, 1], F32, name="seed")
        nc.gpsimd.memset(seed[:], 0.0)
        warm = sb.tile([P, 1], F32, name="warm")
        nc.scalar.activation(warm[:], seed[:], EXP)

        nc.gpsimd.memset(scales[STAGE + 16 : P, :].bitcast(I32), 0)
        nc.vector.memset(scales[0:STAGE, :].bitcast(I32), 0)
        nc.vector.memset(bias_row[0 : P - 1, :], 0.0)
        nc.vector.memset(expo_rows[0 : P - 2, :], 0.0)
        ident = sb.tile([P, P], F32, name="ident")
        make_identity(nc, ident[:])

        def listed(first, count):
            return offsets[:, first // 16 : (first + count) // 16]

        listed_sc = sb.tile([P, N], U8, name="listed_sc", align_bytes=64)
        nc.vector.tensor_copy(listed_sc[:], scales[:].indirect(offsets[:]))
        k_sc = sb.tile([P, N], U8, name="k_sc", align_bytes=64)
        for quad in range(4):
            nc.sync.dma_start(
                out=k_sc[32 * quad : 32 * quad + 4, :].bitcast(I32),
                in_=listed_sc[STAGE + 4 * quad : STAGE + 4 * quad + 4, :].bitcast(I32),
            )

        expo_turned = ps.tile([P, P], F32, name="expo_turned", tag="score0_0")
        nc.tensor.transpose(expo_turned[:], expo_rows[:], ident[:])
        bias_listed = [sb.tile([P, HALF], F32, name=f"bias_listed{h}", tag=f"listed_slot{h}", align_bytes=64) for h in range(2)]
        for h in range(2):
            nc.scalar.activation(bias_listed[h][:], bias_row[:].indirect(listed(h * HALF, HALF)), COPY)
        bias_all = [sb.tile([P, HALF], F32, name=f"bias_all{h}") for h in range(2)]
        spreads = []
        for h in range(2):
            turned = ps.tile([P, 2, P], F32, name="turned", tag=f"bias_bank{h}")
            for s in range(2):
                nc.tensor.transpose(turned[:, s, :], bias_listed[h][:, s * P : (s + 1) * P], ident[:])
            bias_col = sb.tile([P, 2], F32, name=f"bias_col{h}")
            nc.scalar.copy(bias_col[:], turned[:, :, P - 1])
            spread = ps.tile([P, 2, P], F32, name="spread", tag=f"bias_bank{h}")
            for s in range(2):
                nc.tensor.transpose(spread[:, s, :], bias_col[:, s : s + 1].to_broadcast([P, P]), ident[:])
            spreads.append(spread)
        for h in range(2):
            nc.scalar.copy(bias_all[h][:], spreads[h][:].rearrange("p s c -> p (s c)"))

        expo = sb.tile([P, 2], F32, name="expo")
        nc.scalar.copy(expo[:], expo_turned[:, P - 2 : P])

        q_bf = sb.tile([P, NQ, PACK], BF16, name="q_bf", tag="operand_slot", align_bytes=64)
        nc.vector.tensor_copy(
            q_bf[:].rearrange("p (c i) j -> p c j i", i=4), q_raw[:].rearrange("p j (c i) -> p c j i", i=4)
        )
        q_codes = sb.tile([P, NQ], U32, name="q_codes", tag="listed_slot0", align_bytes=64)
        q_sc = sb.tile([P, NQ], U8, name="q_sc", align_bytes=64)
        nc.vector.quantize_mx(
            out=q_codes[:].bitcast(FP8X4), scales=q_sc[:], in_=q_bf[:].rearrange("p m j -> p (m j)")
        )

        k_codes = sb.tile([P, N], U32, name="k_codes", tag="operand_slot", align_bytes=64)
        scores = {}

        def score(t, b, bank):
            cols = slice(b * P, (b + 1) * P)
            tile = ps.tile([P, P], F32, name=f"score{t}_{b}", tag=bank)
            nc.tensor.matmul_mx(
                out=tile[:],
                lhsT=q_codes[:, t * P : (t + 1) * P].bitcast(FP8X4),
                lhsT_scale=q_sc[:, t * P : (t + 1) * P],
                rhs=k_codes[:, cols].bitcast(FP8X4),
                rhs_scale=k_sc[:, cols],
                start=True,
                stop=True,
            )
            scores[t, b] = tile

        for b in range(BLOCKS):
            nc.vector.tensor_copy(
                k_codes[:, b * P : (b + 1) * P], words[:].bitcast(U32).indirect(listed(b * P, P))
            )
        for b in range(BLOCKS - 1):
            for t in range(2):
                score(t, b, f"score{t}_{b}")
        score(0, 3, "bias_bank0")

        rates = [sb.tile([P, N], F32, name=f"rate{t}") for t in range(2)]
        results = [sb.tile([P, N], F32, name=f"res{t}") for t in range(2)]

        def rate(t, b):
            cols = slice(b * P, (b + 1) * P)
            b0 = (b * P) % HALF
            logit = sb.tile([P, P], F32, name=f"logit{t}_{b}")
            nc.vector.tensor_tensor(logit[:], scores[t, b][:], bias_all[b * P // HALF][:, b0 : b0 + P], ADD)
            nc.scalar.activation(rates[t][:, cols], logit[:], EXP)

        def finish(t, first, count):
            cols = slice(first * P, (first + count) * P)
            nc.vector.tensor_scalar(results[t][:, cols], rates[t][:, cols], expo[:, t : t + 1], None, MULT)
            nc.sync.dma_start(out=out[0, t * P : (t + 1) * P, cols], in_=results[t][:, cols])

        rate(0, 0)
        rate(0, 1)
        score(1, 3, "score0_1")
        rate(1, 0)
        rate(1, 1)
        rate(0, 2)
        rate(1, 2)
        finish(0, 0, 2)
        rate(0, 3)
        rate(1, 3)
        finish(1, 0, 2)
        finish(1, 2, 1)
        finish(0, 2, 2)
        finish(1, 3, 1)
